import numpy as np
import ml_dtypes


def mxq(x, axis, fmt="e4m3"):
    dtype, down = {"e4m3": (ml_dtypes.float8_e4m3fn, 7), "e5m2": (ml_dtypes.float8_e5m2, 14)}[fmt]
    v = np.moveaxis(np.asarray(x, np.float32).astype(ml_dtypes.bfloat16).astype(np.float64), axis, -1)
    blocks = v.reshape(v.shape[:-1] + (-1, 32))
    amax = np.abs(blocks).max(-1, keepdims=True)
    byte = np.maximum(np.where(amax > 0, np.frexp(amax)[1] - 1 + 127, 0) - down, 1)
    scale = np.exp2(byte - 127.0)
    codes = (blocks / scale).astype(np.float32).astype(dtype).astype(np.float64)
    return np.moveaxis((codes * scale).reshape(v.shape), -1, axis)


WIDE = False


def mx_kscale(k):
    if not WIDE:
        return np.ones(k)
    levels = np.array([10, -10, 5, -5, 0])
    if k % 512:
        return np.exp2(np.random.permutation(np.resize(levels, k // 32))).repeat(32)
    a = np.empty((k // 512, 16))
    for p in range(k // 512):
        a[p, :8] = np.random.permutation(np.resize(levels, 8))
        for g in range(8):
            far = levels[np.abs(levels - a[p, g]) >= 10]
            a[p, g + 8] = far[np.random.randint(len(far))]
    return np.exp2(a.ravel()).repeat(32)


def f64(x):
    return np.asarray(x).astype(np.float64)


def striped(idx):
    return np.tile(idx.reshape(-1, 16).T, (8, 1)).astype(np.uint16)


def unstriped(offs):
    return offs[:16].T.reshape(-1).astype(np.int64)


E2M1 = np.array([0.0, 0.5, 1.0, 1.5, 2.0, 3.0, 4.0, 6.0, -0.0, -0.5, -1.0, -1.5, -2.0, -3.0, -4.0, -6.0])


def pack_weight(w, fmt):
    k, n = w.shape
    w = f64(np.asarray(w, np.float32).astype(ml_dtypes.bfloat16)).reshape(k // 32, 32, n)
    amax = np.abs(w).max(1)
    if fmt == "e4m3":
        byte = np.frexp(amax)[1] - 1 + 127 - 7
    else:
        mant, ex = np.frexp(amax / 6.0)
        byte = np.where(mant > 0.5, ex, ex - 1) + 127
    byte = np.clip(np.where(amax > 0, byte, 1), 1, 254)
    scaled = (w * np.exp2(127.0 - byte)[:, None, :]).reshape(k, n).astype(np.float32)
    by_word = np.ascontiguousarray(scaled.reshape(k // 512, 128, 4, n).transpose(0, 1, 3, 2))
    if fmt == "e4m3":
        words = by_word.astype(ml_dtypes.float8_e4m3fn).view(np.uint8)
    else:
        c = by_word.astype(ml_dtypes.float4_e2m1fn).view(np.uint8) & 0xF
        words = (c[..., 0::2] | (c[..., 1::2] << 4)).reshape(k // 512, 128, 2 * n)
    return np.ascontiguousarray(words), np.ascontiguousarray(byte.astype(np.uint8).reshape(k // 512, 16, n))


def unpack_weight(words, scales, fmt):
    g, _, n = scales.shape
    words = np.ascontiguousarray(words).reshape(g, 128, n, -1)
    if fmt == "e4m3":
        vals = words.view(ml_dtypes.float8_e4m3fn).astype(np.float64)
    else:
        nib = np.empty((g, 128, n, 4), np.uint8)
        nib[..., 0::2] = words & 0xF
        nib[..., 1::2] = words >> 4
        vals = E2M1[nib]
    vals = vals * np.repeat(np.exp2(scales.astype(np.float64) - 127.0), 8, axis=1)[..., None]
    return vals.transpose(0, 1, 3, 2).reshape(g * 512, n)


def gelu(v):
    return 0.5 * v * (1.0 + np.tanh(np.sqrt(2.0 / np.pi) * (v + 0.044715 * v**3)))


K, T, S, H, T2, P = 1024, 2048, 1024, 512, 2048, 1024

def setup_inputs():
    n = np.random.standard_normal
    s = mx_kscale(K)[:, None]
    u = mx_kscale(H)[:, None]
    tab_words, tab_scales = pack_weight(n((K, T)) * s, "e4m3")
    w4_words, w4_scales = pack_weight(n((K, H)) / np.sqrt(K) / s * u.T, "e2m1")
    return {
        "tab_words": tab_words, "tab_scales": tab_scales,
        "offs": striped(np.random.permutation(T)[:S]),
        "w1": (n((K, H)) / np.sqrt(K) / s * u.T).astype(np.float32),
        "w4_words": w4_words, "w4_scales": w4_scales,
        "page0": (n((H, T2)) * u).astype(np.float32),
        "wgs": np.exp(0.3 * n((128, S))).astype(np.float32),
        "offs2": striped(np.random.permutation(T2)[:S]),
        "shift": (0.8 * n(H) * u[:, 0]).astype(np.float32),
        "offs3": striped(np.random.permutation(T2)[:P]),
        "w2": (n((H, H)) / np.sqrt(H) / u * u.T).astype(np.float32),
        "expo": np.exp(0.4 * n((H, P))).astype(np.float32),
        "wgo": np.exp(0.3 * n((128, P))).astype(np.float32),
        "offs4": striped(np.random.permutation(T2)[:P]),
    }

def reference(tab_words, tab_scales, offs, w1, w4_words, w4_scales, page0, wgs, offs2,
              shift, offs3, w2, expo, wgo, offs4):
    v = unpack_weight(tab_words, tab_scales, "e4m3")[:, unstriped(offs)]
    w4 = unpack_weight(w4_words, w4_scales, "e2m1")
    flap = mxq(f64(w1), 0, "e4m3").T @ v
    edge = w4.T @ v
    h = np.maximum(flap, edge)
    page = f64(page0).copy()
    page[:, unstriped(offs2)] = np.tile(f64(wgs), (H // 128, 1)) * h
    x = np.abs(page[:, unstriped(offs3)] + f64(shift)[:, None])
    y = mxq(f64(w2), 0, "e4m3").T @ mxq(x, 0, "e4m3")
    y = f64(expo) * y
    page[:, unstriped(offs4)] = np.tile(f64(wgo), (H // 128, 1)) * y
    return page

@@ -1,0 +1,278 @@
+from contextlib import ExitStack
+
+import concourse.mybir as mybir
+from concourse.masks import make_identity
+
+K, T, S, H, T2, NP = 1024, 2048, 1024, 512, 2048, 1024
+FLOPS = 2 * (2 * K * H * S + H * H * NP)
+
+F32 = mybir.dt.float32
+BF16 = mybir.dt.bfloat16
+I32 = mybir.dt.int32
+U32 = mybir.dt.uint32
+U16 = mybir.dt.uint16
+U8 = mybir.dt.uint8
+FP8X4 = mybir.dt.float8_e4m3fn_x4
+FP4X4 = mybir.dt.float4_e2m1fn_x4
+MULT = mybir.AluOpType.mult
+MAX = mybir.AluOpType.max
+ABS = mybir.ActivationFunctionType.Abs
+
+P = 128
+PASSES = K // 512
+TILES = H // P
+BANK = 512
+QUARTER = 256
+
+
+def tile_list_pitch_bearing_register_kernel(
+    tc, tab_words, tab_scales, offs, w1, w4_words, w4_scales, page0, wgs, offs2,
+    shift, offs3, w2, expo, wgo, offs4, out,
+):
+    nc = tc.nc
+    with ExitStack() as ctx:
+        keep = ctx.enter_context(tc.tile_pool(name="keep", bufs=1))
+        ring = ctx.enter_context(tc.tile_pool(name="ring", bufs=2))
+        psum = ctx.enter_context(tc.psum_pool(name="psum", bufs=1))
+
+        def held(shape, dtype, name):
+            return keep.tile(shape, dtype, name=name, align_bytes=64)
+
+        def bank(shape, dtype, tag):
+            return psum.tile(shape, dtype, name=tag, tag=tag)
+
+        def entries(lst, first, count):
+            return lst[:, first // 16 : (first + count) // 16]
+
+        lst1 = keep.tile([P, S // 16], U16, name="lst1")
+        lst2 = keep.tile([P, S // 16], U16, name="lst2")
+        lst3 = keep.tile([P, NP // 16], U16, name="lst3")
+        lst4 = keep.tile([P, NP // 16], U16, name="lst4")
+
+        tab_sc = held([P, T], U8, "tab_sc")
+        w4_sc = held([P, PASSES, H], U8, "w4_sc")
+        v_sc1 = held([P, S], U8, "v_sc1")
+        nc.gpsimd.memset(tab_sc[:].bitcast(I32), 0)
+        nc.vector.memset(w4_sc[:].rearrange("p a c -> p (a c)").bitcast(I32), 0)
+        nc.vector.memset(v_sc1[:].bitcast(I32), 0)
+
+        ident_bf = held([P, P], BF16, "ident_bf")
+        ident_f32 = held([P, P], F32, "ident_f32")
+        make_identity(nc, ident_bf[:])
+        make_identity(nc, ident_f32[:])
+
+        tab = [held([P, T], U32, f"tab{a}") for a in range(PASSES)]
+        w1_k = w1.rearrange("(a p j) c -> a p j c", p=P, j=4)
+        w1_groups = ((0, 1), (1, 2), (2, 4))
+        w1_raw = [held([P, PASSES, 4, P * (hi - lo)], F32, f"w1_raw{lo}") for lo, hi in w1_groups]
+        w4_w = held([P, PASSES, 2 * H], U8, "w4_w")
+        page = [held([P, T2], F32, f"page{n}") for n in range(TILES)]
+        wgs_sb = held([P, S], F32, "wgs_sb")
+        wgo_sb = held([P, NP], F32, "wgo_sb")
+        expo_sb = [held([P, NP], F32, f"expo{n}") for n in range(TILES)]
+        w2_raw = held([P, 4, H], F32, "w2_raw")
+        shift_sb = held([P, TILES], F32, "shift_sb")
+
+        def load_w1(g):
+            lo, hi = w1_groups[g]
+            for a in range(PASSES):
+                nc.sync.dma_start(out=w1_raw[g][:, a], in_=w1_k[a][:, :, P * lo : P * hi])
+
+        def rows(n):
+            return slice(P * n, P * (n + 1))
+
+        nc.sync.dma_start(lst1[:], offs)
+
+        def load_tab(a):
+            nc.sync.dma_start(
+                out=tab[a][:].bitcast(I32),
+                in_=tab_words[a].rearrange("p t i -> p (t i)").bitcast(I32),
+            )
+
+        load_tab(0)
+        load_w1(0)
+        for q in range(4):
+            nc.sync.dma_start(
+                out=tab_sc[32 * q : 32 * q + 8, :].bitcast(I32),
+                in_=tab_scales[:, 4 * q : 4 * q + 4, :].bitcast(I32),
+            )
+        load_tab(1)
+        for q in range(4):
+            nc.sync.dma_start(
+                out=w4_sc[32 * q : 32 * q + 4, :, :].bitcast(I32),
+                in_=w4_scales[:, 4 * q : 4 * q + 4, :].rearrange("a r c -> r a c").bitcast(I32),
+            )
+        nc.sync.dma_start(out=w4_w[:].bitcast(I32), in_=w4_words.rearrange("a p c -> p a c").bitcast(I32))
+        nc.sync.dma_start(lst2[:], offs2)
+        nc.sync.dma_start(out=page[0][:], in_=page0[rows(0), :])
+        nc.sync.dma_start(out=wgs_sb[:, :BANK], in_=wgs[:, :BANK])
+        load_w1(1)
+        load_w1(2)
+        nc.sync.dma_start(out=wgs_sb[:, BANK:], in_=wgs[:, BANK:])
+        nc.sync.dma_start(lst3[:], offs3)
+        nc.sync.dma_start(out=page[1][:], in_=page0[rows(1), :])
+        with nc.allow_non_contiguous_dma(reason="one shift value to a partition"):
+            nc.sync.dma_start(out=shift_sb[:], in_=shift.rearrange("(n p) -> p n", p=P))
+        nc.sync.dma_start(out=wgo_sb[:], in_=wgo)
+        nc.sync.dma_start(out=expo_sb[0][:], in_=expo[rows(0), :])
+        nc.sync.dma_start(out=page[2][:], in_=page0[rows(2), :])
+        nc.sync.dma_start(out=w2_raw[:], in_=w2.rearrange("(p j) c -> p j c", j=4))
+        for n in range(1, TILES):
+            nc.sync.dma_start(out=expo_sb[n][:], in_=expo[rows(n), :])
+        nc.sync.dma_start(lst4[:], offs4)
+        nc.sync.dma_start(out=page[3][:], in_=page0[rows(3), :])
+
+        v_sc = held([P, S], U8, "v_sc")
+        v_w = {}
+
+        def pick_words(a, half, tag):
+            words = keep.tile([P, BANK], U32, name="words", tag=tag, align_bytes=64)
+            nc.vector.tensor_copy(words[:], tab[a][:].indirect(entries(lst1, BANK * half, BANK)))
+            v_w[a, half] = words
+
+        pick_words(0, 0, "v_w00")
+        nc.vector.tensor_copy(v_sc[:], tab_sc[:].indirect(lst1[:]))
+        nc.scalar.dma_start(out=v_sc1[0:100, :].bitcast(I32), in_=v_sc[4:104, :].bitcast(I32))
+
+        w1_q, w1_sc = [], []
+        for n in range(TILES):
+            g = min(n, 2)
+            first = P * (n - w1_groups[g][0])
+            woven = keep.tile([P, PASSES, P, 4], BF16, name="w1_woven", tag=f"w1_woven{n}", align_bytes=64)
+            nc.scalar.copy(woven[:], w1_raw[g][:, :, :, first : first + P].rearrange("p a j c -> p a c j"))
+            codes = held([P, PASSES * P], U32, f"w1_q{n}")
+            scales = held([P, PASSES * P], U8, f"w1_sc{n}")
+            nc.vector.quantize_mx(codes[:].bitcast(FP8X4), scales[:], woven[:].rearrange("p a c j -> p (a c j)"))
+            w1_q.append(codes)
+            w1_sc.append(scales)
+            if n == 0:
+                pick_words(1, 0, "v_w10")
+                pick_words(0, 1, "w1_woven0")
+                pick_words(1, 1, "v_w11")
+
+        x_t = held([P, NP // P, 2, P], F32, "x_t")
+        weight_y = {}
+
+        def turn(n, picked, first, count):
+            blocks = count // P
+            size = ring.tile([P, count], BF16, name="size", tag=f"size{count}", align_bytes=64)
+            nc.scalar.activation(size[:], picked, ABS, bias=shift_sb[:, n : n + 1])
+            turned = psum.tile([P, blocks, P], BF16, name="turned", tag="turned", bufs=2)
+            for b in range(blocks):
+                nc.tensor.transpose(turned[:, b, :], size[:, P * b : P * (b + 1)], ident_bf[:])
+            nc.scalar.copy(
+                x_t[:, first // P : first // P + blocks, :, 32 * n : 32 * (n + 1)],
+                turned[:].bitcast(F32).rearrange("j b (m u) -> j b u m", u=2),
+            )
+
+        def pick(n, first, count, tag):
+            picked = keep.tile([P, count], F32, name="picked", tag=tag, align_bytes=64)
+            lst = lst3[:] if count == NP else entries(lst3, first, count)
+            nc.vector.tensor_copy(picked[:], page[n][:].indirect(lst))
+            return picked
+
+        def make_factor(n, tag):
+            factor = keep.tile([P, NP], F32, name="factor", tag=tag, align_bytes=64)
+            nc.vector.tensor_tensor(factor[:], expo_sb[n][:], wgo_sb[:], MULT)
+            weight_y[n] = factor
+
+        for n in range(TILES):
+            h = keep.tile([P, S], F32, name="h", tag=f"h{n}", align_bytes=64)
+            flap_sb = keep.tile([P, S], F32, name="flap_sb", tag=f"flap_sb{n}", align_bytes=64)
+            for half in range(2):
+                cols = slice(BANK * half, BANK * (half + 1))
+                edge = bank([P, BANK], F32, f"edge{half}")
+                flap = bank([P, BANK], F32, f"flap{half}")
+                for a in range(PASSES):
+                    nc.tensor.matmul_mx(
+                        out=flap[:],
+                        lhsT=w1_q[n][:, rows(a)].bitcast(FP8X4),
+                        lhsT_scale=w1_sc[n][:, rows(a)],
+                        rhs=v_w[a, half][:].bitcast(FP8X4),
+                        rhs_scale=v_sc[4 * a :, cols],
+                        start=(a == 0), stop=(a == PASSES - 1),
+                    )
+                for a in range(PASSES):
+                    nc.tensor.matmul_mx(
+                        out=edge[:],
+                        lhsT=w4_w[:, a, 2 * P * n : 2 * P * (n + 1)].bitcast(FP4X4),
+                        lhsT_scale=w4_sc[:, a, rows(n)],
+                        rhs=v_w[a, half][:].bitcast(FP8X4),
+                        rhs_scale=(v_sc, v_sc1)[a][:, cols],
+                        start=(a == 0), stop=(a == PASSES - 1),
+                    )
+                nc.scalar.copy(flap_sb[:, cols], flap[:])
+                nc.vector.tensor_tensor(h[:, cols], edge[:], flap_sb[:, cols], MAX)
+                if n == 0:
+                    nc.vector.tensor_tensor(
+                        page[n][:].indirect(entries(lst2, BANK * half, BANK)), h[:, cols], wgs_sb[:, cols], MULT
+                    )
+            if n > 0:
+                turn(n - 1, pick(n - 1, 0, NP, f"flap_sb{n}")[:], 0, NP)
+                nc.vector.tensor_tensor(page[n][:].indirect(lst2[:]), h[:], wgs_sb[:], MULT)
+            if n < 2:
+                make_factor(n, f"h{n}")
+
+        w2_woven = held([P, H, 4], BF16, "w2_woven")
+        nc.scalar.copy(w2_woven[:], w2_raw[:].rearrange("p j c -> p c j"))
+        w2_q = held([P, H], U32, "w2_q")
+        w2_sc = held([P, H], U8, "w2_sc")
+        nc.vector.quantize_mx(w2_q[:].bitcast(FP8X4), w2_sc[:], w2_woven[:].rearrange("p c j -> p (c j)"))
+
+        last = TILES - 1
+        x_q = held([P, NP], U32, "x_q")
+        x_sc = held([P, NP], U8, "x_sc")
+        for first in range(0, NP, QUARTER):
+            turn(last, pick(last, first, QUARTER, f"picked{first}")[:], first, QUARTER)
+            back = bank([P, QUARTER // P, 2, P], F32, f"back{first // QUARTER % 2}")
+            for b in range(QUARTER // P):
+                for u in range(2):
+                    nc.tensor.transpose(back[:, b, u, :], x_t[:, first // P + b, u, :], ident_f32[:])
+            x_woven = keep.tile([P, QUARTER, 4], BF16, name="x_woven", tag=f"x_woven{first}", align_bytes=64)
+            nc.scalar.copy(
+                x_woven[:].bitcast(F32).rearrange("p (b j) u -> p b j u", j=P),
+                back[:].rearrange("p b u j -> p b j u"),
+            )
+            nc.vector.quantize_mx(
+                x_q[:, first : first + QUARTER].bitcast(FP8X4),
+                x_sc[:, first : first + QUARTER],
+                x_woven[:].rearrange("p j t -> p (j t)"),
+            )
+        make_factor(last, f"h{last}")
+        make_factor(2, "x_woven0")
+
+        y_sb = [held([P, NP], F32, f"y{n}") for n in range(TILES)]
+
+        def score(n, first, count, tag):
+            cols = slice(first, first + count)
+            acc = bank([P, count], F32, tag)
+            nc.tensor.matmul_mx(
+                out=acc[:],
+                lhsT=w2_q[:, rows(n)].bitcast(FP8X4), lhsT_scale=w2_sc[:, rows(n)],
+                rhs=x_q[:, cols].bitcast(FP8X4), rhs_scale=x_sc[:, cols],
+                start=True, stop=True,
+            )
+            nc.scalar.copy(y_sb[n][:, cols], acc[:])
+
+        def put(n, first, count):
+            cols = slice(first, first + count)
+            lst = lst4[:] if count == NP else entries(lst4, first, count)
+            nc.vector.tensor_tensor(page[n][:].indirect(lst), y_sb[n][:, cols], weight_y[n][:, cols], MULT)
+
+        def store(n):
+            nc.sync.dma_start(out=out[rows(n), :], in_=page[n][:])
+
+        for first in (0, QUARTER):
+            for n in (0, 1):
+                score(n, first, QUARTER, ("edge0", "flap0")[n] if first == 0 else ("edge1", "flap1")[n])
+                put(n, first, QUARTER)
+        score(2, 0, BANK, "back1")
+        put(2, 0, BANK)
+        for n in range(3):
+            score(n, BANK, BANK, ("edge0", "flap0", "edge1")[n])
+            put(n, BANK, BANK)
+            store(n)
+        score(3, 0, BANK, "flap1")
+        score(3, BANK, BANK, "back0")
+        put(3, 0, NP)
+        store(3)

@@ -32,6 +32,7 @@ def tile_list_pitch_bearing_register_kernel(
     nc = tc.nc
     with ExitStack() as ctx:
         keep = ctx.enter_context(tc.tile_pool(name="keep", bufs=1))
+        late = ctx.enter_context(tc.tile_pool(name="late", bufs=1))
         ring = ctx.enter_context(tc.tile_pool(name="ring", bufs=2))
         psum = ctx.enter_context(tc.psum_pool(name="psum", bufs=1))
 
@@ -58,8 +59,8 @@ def tile_list_pitch_bearing_register_kernel(
 
         ident_bf = held([P, P], BF16, "ident_bf")
         ident_f32 = held([P, P], F32, "ident_f32")
-        make_identity(nc, ident_bf[:])
         make_identity(nc, ident_f32[:])
+        nc.scalar.activation(ident_bf[:], ident_f32[:], ABS)
 
         tab = [held([P, T], U32, f"tab{a}") for a in range(PASSES)]
         w1_k = w1.rearrange("(a p j) c -> a p j c", p=P, j=4)
@@ -67,7 +68,7 @@ def tile_list_pitch_bearing_register_kernel(
         w1_raw = [held([P, PASSES, 4, P * (hi - lo)], F32, f"w1_raw{lo}") for lo, hi in w1_groups]
         w4_w = held([P, PASSES, 2 * H], U8, "w4_w")
         page = [held([P, T2], F32, f"page{n}") for n in range(TILES)]
-        wgs_sb = held([P, S], F32, "wgs_sb")
+        wgs_sb = keep.tile([P, S], F32, name="wgs_sb", tag="wgs_sb", align_bytes=64)
         wgo_sb = held([P, NP], F32, "wgo_sb")
         expo_sb = [held([P, NP], F32, f"expo{n}") for n in range(TILES)]
         w2_raw = held([P, 4, H], F32, "w2_raw")
@@ -82,6 +83,8 @@ def tile_list_pitch_bearing_register_kernel(
             return slice(P * n, P * (n + 1))
 
         nc.sync.dma_start(lst1[:], offs)
+        nc.sync.dma_start(lst2[:], offs2)
+        nc.sync.dma_start(lst3[:], offs3)
 
         def load_tab(a):
             nc.sync.dma_start(
@@ -89,13 +92,13 @@ def tile_list_pitch_bearing_register_kernel(
                 in_=tab_words[a].rearrange("p t i -> p (t i)").bitcast(I32),
             )
 
-        load_tab(0)
-        load_w1(0)
         for q in range(4):
             nc.sync.dma_start(
                 out=tab_sc[32 * q : 32 * q + 8, :].bitcast(I32),
                 in_=tab_scales[:, 4 * q : 4 * q + 4, :].bitcast(I32),
             )
+        load_tab(0)
+        load_w1(0)
         load_tab(1)
         for q in range(4):
             nc.sync.dma_start(
@@ -103,21 +106,18 @@ def tile_list_pitch_bearing_register_kernel(
                 in_=w4_scales[:, 4 * q : 4 * q + 4, :].rearrange("a r c -> r a c").bitcast(I32),
             )
         nc.sync.dma_start(out=w4_w[:].bitcast(I32), in_=w4_words.rearrange("a p c -> p a c").bitcast(I32))
-        nc.sync.dma_start(lst2[:], offs2)
         nc.sync.dma_start(out=page[0][:], in_=page0[rows(0), :])
         nc.sync.dma_start(out=wgs_sb[:, :BANK], in_=wgs[:, :BANK])
         load_w1(1)
         load_w1(2)
         nc.sync.dma_start(out=wgs_sb[:, BANK:], in_=wgs[:, BANK:])
-        nc.sync.dma_start(lst3[:], offs3)
         nc.sync.dma_start(out=page[1][:], in_=page0[rows(1), :])
+        nc.sync.dma_start(out=page[2][:], in_=page0[rows(2), :])
         with nc.allow_non_contiguous_dma(reason="one shift value to a partition"):
             nc.sync.dma_start(out=shift_sb[:], in_=shift.rearrange("(n p) -> p n", p=P))
-        nc.sync.dma_start(out=wgo_sb[:], in_=wgo)
-        nc.sync.dma_start(out=expo_sb[0][:], in_=expo[rows(0), :])
-        nc.sync.dma_start(out=page[2][:], in_=page0[rows(2), :])
         nc.sync.dma_start(out=w2_raw[:], in_=w2.rearrange("(p j) c -> p j c", j=4))
-        for n in range(1, TILES):
+        nc.sync.dma_start(out=wgo_sb[:], in_=wgo)
+        for n in range(TILES):
             nc.sync.dma_start(out=expo_sb[n][:], in_=expo[rows(n), :])
         nc.sync.dma_start(lst4[:], offs4)
         nc.sync.dma_start(out=page[3][:], in_=page0[rows(3), :])
@@ -130,9 +130,9 @@ def tile_list_pitch_bearing_register_kernel(
             nc.vector.tensor_copy(words[:], tab[a][:].indirect(entries(lst1, BANK * half, BANK)))
             v_w[a, half] = words
 
-        pick_words(0, 0, "v_w00")
         nc.vector.tensor_copy(v_sc[:], tab_sc[:].indirect(lst1[:]))
-        nc.scalar.dma_start(out=v_sc1[0:100, :].bitcast(I32), in_=v_sc[4:104, :].bitcast(I32))
+        pick_words(0, 0, "v_w00")
+        nc.gpsimd.dma_start(out=v_sc1[0:100, :].bitcast(I32), in_=v_sc[4:104, :].bitcast(I32))
 
         w1_q, w1_sc = [], []
         for n in range(TILES):
@@ -153,9 +153,10 @@ def tile_list_pitch_bearing_register_kernel(
         x_t = held([P, NP // P, 2, P], F32, "x_t")
         weight_y = {}
 
-        def turn(n, picked, first, count):
+        def turn(n, picked, first, count, size=None):
             blocks = count // P
-            size = ring.tile([P, count], BF16, name="size", tag=f"size{count}", align_bytes=64)
+            if size is None:
+                size = ring.tile([P, count], BF16, name="size", tag=f"size{count}", align_bytes=64)
             nc.scalar.activation(size[:], picked, ABS, bias=shift_sb[:, n : n + 1])
             turned = psum.tile([P, blocks, P], BF16, name="turned", tag="turned", bufs=2)
             for b in range(blocks):
@@ -171,9 +172,8 @@ def tile_list_pitch_bearing_register_kernel(
             nc.vector.tensor_copy(picked[:], page[n][:].indirect(lst))
             return picked
 
-        def make_factor(n, tag):
-            factor = keep.tile([P, NP], F32, name="factor", tag=tag, align_bytes=64)
-            nc.vector.tensor_tensor(factor[:], expo_sb[n][:], wgo_sb[:], MULT)
+        def make_factor(n, engine, factor):
+            engine.tensor_tensor(factor[:], expo_sb[n][:], wgo_sb[:], MULT)
             weight_y[n] = factor
 
         for n in range(TILES):
@@ -210,25 +210,20 @@ def tile_list_pitch_bearing_register_kernel(
             if n > 0:
                 turn(n - 1, pick(n - 1, 0, NP, f"flap_sb{n}")[:], 0, NP)
                 nc.vector.tensor_tensor(page[n][:].indirect(lst2[:]), h[:], wgs_sb[:], MULT)
-            if n < 2:
-                make_factor(n, f"h{n}")
+                make_factor(n - 1, nc.gpsimd, keep.tile([P, NP], F32, name="factor", tag=f"h{n}", align_bytes=64))
 
         w2_woven = held([P, H, 4], BF16, "w2_woven")
         nc.scalar.copy(w2_woven[:], w2_raw[:].rearrange("p j c -> p c j"))
-        w2_q = held([P, H], U32, "w2_q")
-        w2_sc = held([P, H], U8, "w2_sc")
-        nc.vector.quantize_mx(w2_q[:].bitcast(FP8X4), w2_sc[:], w2_woven[:].rearrange("p c j -> p (c j)"))
 
         last = TILES - 1
         x_q = held([P, NP], U32, "x_q")
         x_sc = held([P, NP], U8, "x_sc")
-        for first in range(0, NP, QUARTER):
-            turn(last, pick(last, first, QUARTER, f"picked{first}")[:], first, QUARTER)
+
+        def turn_back(first, x_woven):
             back = bank([P, QUARTER // P, 2, P], F32, f"back{first // QUARTER % 2}")
             for b in range(QUARTER // P):
                 for u in range(2):
                     nc.tensor.transpose(back[:, b, u, :], x_t[:, first // P + b, u, :], ident_f32[:])
-            x_woven = keep.tile([P, QUARTER, 4], BF16, name="x_woven", tag=f"x_woven{first}", align_bytes=64)
             nc.scalar.copy(
                 x_woven[:].bitcast(F32).rearrange("p (b j) u -> p b j u", j=P),
                 back[:].rearrange("p b u j -> p b j u"),
@@ -238,8 +233,16 @@ def tile_list_pitch_bearing_register_kernel(
                 x_sc[:, first : first + QUARTER],
                 x_woven[:].rearrange("p j t -> p (j t)"),
             )
-        make_factor(last, f"h{last}")
-        make_factor(2, "x_woven0")
+
+        picked = [pick(last, first, count, f"picked{first}") for first, count in ((0, QUARTER), (QUARTER, QUARTER), (BANK, BANK))]
+        w2_q = keep.tile([P, H], U32, name="w2_q", tag="wgs_sb", align_bytes=64)
+        w2_sc = held([P, H], U8, "w2_sc")
+        nc.vector.quantize_mx(w2_q[:].bitcast(FP8X4), w2_sc[:], w2_woven[:].rearrange("p c j -> p (c j)"))
+        turn(last, picked[0][:], 0, QUARTER)
+        turn_back(0, late.tile([P, QUARTER, 4], BF16, name="x_woven0", offset=0, align_bytes=64))
+        turn(last, picked[1][:], QUARTER, QUARTER)
+        turn_back(QUARTER, held([P, QUARTER, 4], BF16, "x_woven1"))
+        make_factor(last, nc.vector, late.tile([P, NP], F32, name="factor3", offset=1024, align_bytes=64))
 
         y_sb = [held([P, NP], F32, f"y{n}") for n in range(TILES)]
 
@@ -266,6 +269,9 @@ def tile_list_pitch_bearing_register_kernel(
             for n in (0, 1):
                 score(n, first, QUARTER, ("edge0", "flap0")[n] if first == 0 else ("edge1", "flap1")[n])
                 put(n, first, QUARTER)
+        turn(last, picked[2][:], BANK, BANK, late.tile([P, BANK], BF16, name="size_late", offset=0, align_bytes=64))
+        for first in (BANK, BANK + QUARTER):
+            turn_back(first, held([P, QUARTER, 4], BF16, f"x_woven{first}"))
         score(2, 0, BANK, "back1")
         put(2, 0, BANK)
         for n in range(3):

@@ -33,6 +33,7 @@ def tile_list_pitch_bearing_register_kernel(
     with ExitStack() as ctx:
         keep = ctx.enter_context(tc.tile_pool(name="keep", bufs=1))
         late = ctx.enter_context(tc.tile_pool(name="late", bufs=1))
+        mid = ctx.enter_context(tc.tile_pool(name="mid", bufs=1))
         ring = ctx.enter_context(tc.tile_pool(name="ring", bufs=2))
         psum = ctx.enter_context(tc.psum_pool(name="psum", bufs=1))
 
@@ -55,12 +56,12 @@ def tile_list_pitch_bearing_register_kernel(
         v_sc1 = held([P, S], U8, "v_sc1")
         nc.gpsimd.memset(tab_sc[:].bitcast(I32), 0)
         nc.vector.memset(w4_sc[:].rearrange("p a c -> p (a c)").bitcast(I32), 0)
-        nc.vector.memset(v_sc1[:].bitcast(I32), 0)
 
         ident_bf = held([P, P], BF16, "ident_bf")
         ident_f32 = held([P, P], F32, "ident_f32")
         make_identity(nc, ident_f32[:])
         nc.scalar.activation(ident_bf[:], ident_f32[:], ABS)
+        nc.gpsimd.memset(v_sc1[:].bitcast(I32), 0)
 
         tab = [held([P, T], U32, f"tab{a}") for a in range(PASSES)]
         w1_k = w1.rearrange("(a p j) c -> a p j c", p=P, j=4)
@@ -97,15 +98,18 @@ def tile_list_pitch_bearing_register_kernel(
                 out=tab_sc[32 * q : 32 * q + 8, :].bitcast(I32),
                 in_=tab_scales[:, 4 * q : 4 * q + 4, :].bitcast(I32),
             )
+        v_sc = held([P, S], U8, "v_sc")
+        nc.vector.tensor_copy(v_sc[:], tab_sc[:].indirect(lst1[:]))
         load_tab(0)
         load_w1(0)
-        load_tab(1)
+        nc.sync.dma_start(out=w4_w[:].bitcast(I32), in_=w4_words.rearrange("a p c -> p a c").bitcast(I32))
         for q in range(4):
             nc.sync.dma_start(
                 out=w4_sc[32 * q : 32 * q + 4, :, :].bitcast(I32),
                 in_=w4_scales[:, 4 * q : 4 * q + 4, :].rearrange("a r c -> r a c").bitcast(I32),
             )
-        nc.sync.dma_start(out=w4_w[:].bitcast(I32), in_=w4_words.rearrange("a p c -> p a c").bitcast(I32))
+        load_tab(1)
+        nc.sync.dma_start(out=v_sc1[0:100, :].bitcast(I32), in_=v_sc[4:104, :].bitcast(I32))
         nc.sync.dma_start(out=page[0][:], in_=page0[rows(0), :])
         nc.sync.dma_start(out=wgs_sb[:, :BANK], in_=wgs[:, :BANK])
         load_w1(1)
@@ -122,33 +126,23 @@ def tile_list_pitch_bearing_register_kernel(
         nc.sync.dma_start(lst4[:], offs4)
         nc.sync.dma_start(out=page[3][:], in_=page0[rows(3), :])
 
-        v_sc = held([P, S], U8, "v_sc")
-        v_w = {}
-
-        def pick_words(a, half, tag):
-            words = keep.tile([P, BANK], U32, name="words", tag=tag, align_bytes=64)
-            nc.vector.tensor_copy(words[:], tab[a][:].indirect(entries(lst1, BANK * half, BANK)))
-            v_w[a, half] = words
-
-        nc.vector.tensor_copy(v_sc[:], tab_sc[:].indirect(lst1[:]))
-        pick_words(0, 0, "v_w00")
-        nc.gpsimd.dma_start(out=v_sc1[0:100, :].bitcast(I32), in_=v_sc[4:104, :].bitcast(I32))
+        v_w = [held([P, S], U32, f"v_w{a}") for a in range(PASSES)]
+        nc.vector.tensor_copy(v_w[0][:], tab[0][:].indirect(lst1[:]))
 
         w1_q, w1_sc = [], []
         for n in range(TILES):
             g = min(n, 2)
             first = P * (n - w1_groups[g][0])
-            woven = keep.tile([P, PASSES, P, 4], BF16, name="w1_woven", tag=f"w1_woven{n}", align_bytes=64)
+            woven = keep.tile([P, PASSES, P, 4], BF16, name="woven", tag=f"w1_woven{n}", align_bytes=64)
             nc.scalar.copy(woven[:], w1_raw[g][:, :, :, first : first + P].rearrange("p a j c -> p a c j"))
             codes = held([P, PASSES * P], U32, f"w1_q{n}")
             scales = held([P, PASSES * P], U8, f"w1_sc{n}")
             nc.vector.quantize_mx(codes[:].bitcast(FP8X4), scales[:], woven[:].rearrange("p a c j -> p (a c j)"))
-            w1_q.append(codes)
-            w1_sc.append(scales)
+            w1_q.append([codes[:, rows(a)] for a in range(PASSES)])
+            w1_sc.append([scales[:, rows(a)] for a in range(PASSES)])
             if n == 0:
-                pick_words(1, 0, "v_w10")
-                pick_words(0, 1, "w1_woven0")
-                pick_words(1, 1, "v_w11")
+                for first in (0, BANK):
+                    nc.vector.tensor_copy(v_w[1][:, first : first + BANK], tab[1][:].indirect(entries(lst1, first, BANK)))
 
         x_t = held([P, NP // P, 2, P], F32, "x_t")
         weight_y = {}
@@ -166,8 +160,7 @@ def tile_list_pitch_bearing_register_kernel(
                 turned[:].bitcast(F32).rearrange("j b (m u) -> j b u m", u=2),
             )
 
-        def pick(n, first, count, tag):
-            picked = keep.tile([P, count], F32, name="picked", tag=tag, align_bytes=64)
+        def pick(n, first, count, picked):
             lst = lst3[:] if count == NP else entries(lst3, first, count)
             nc.vector.tensor_copy(picked[:], page[n][:].indirect(lst))
             return picked
@@ -178,17 +171,21 @@ def tile_list_pitch_bearing_register_kernel(
 
         for n in range(TILES):
             h = keep.tile([P, S], F32, name="h", tag=f"h{n}", align_bytes=64)
-            flap_sb = keep.tile([P, S], F32, name="flap_sb", tag=f"flap_sb{n}", align_bytes=64)
+            if n == 2:
+                flap_sb = mid.tile([P, S], F32, name="flap_sb2", offset=0, align_bytes=64)
+            else:
+                flap_sb = keep.tile([P, S], F32, name="flap_sb", tag=f"flap_sb{n}", align_bytes=64)
             for half in range(2):
                 cols = slice(BANK * half, BANK * (half + 1))
-                edge = bank([P, BANK], F32, f"edge{half}")
-                flap = bank([P, BANK], F32, f"flap{half}")
+                pair = 0 if n == 0 else 1 - half
+                edge = bank([P, BANK], F32, f"edge{pair}")
+                flap = bank([P, BANK], F32, f"flap{pair}")
                 for a in range(PASSES):
                     nc.tensor.matmul_mx(
                         out=flap[:],
-                        lhsT=w1_q[n][:, rows(a)].bitcast(FP8X4),
-                        lhsT_scale=w1_sc[n][:, rows(a)],
-                        rhs=v_w[a, half][:].bitcast(FP8X4),
+                        lhsT=w1_q[n][a].bitcast(FP8X4),
+                        lhsT_scale=w1_sc[n][a],
+                        rhs=v_w[a][:, cols].bitcast(FP8X4),
                         rhs_scale=v_sc[4 * a :, cols],
                         start=(a == 0), stop=(a == PASSES - 1),
                     )
@@ -197,20 +194,29 @@ def tile_list_pitch_bearing_register_kernel(
                         out=edge[:],
                         lhsT=w4_w[:, a, 2 * P * n : 2 * P * (n + 1)].bitcast(FP4X4),
                         lhsT_scale=w4_sc[:, a, rows(n)],
-                        rhs=v_w[a, half][:].bitcast(FP8X4),
+                        rhs=v_w[a][:, cols].bitcast(FP8X4),
                         rhs_scale=(v_sc, v_sc1)[a][:, cols],
                         start=(a == 0), stop=(a == PASSES - 1),
                     )
                 nc.scalar.copy(flap_sb[:, cols], flap[:])
-                nc.vector.tensor_tensor(h[:, cols], edge[:], flap_sb[:, cols], MAX)
+                larger = h[:, cols]
+                if (n, half) == (0, 1):
+                    h_late = keep.tile([P, BANK], F32, name="h_late", tag="w1_woven1", align_bytes=64)
+                    larger = h_late[:]
+                nc.vector.tensor_tensor(larger, edge[:], flap_sb[:, cols], MAX)
                 if n == 0:
                     nc.vector.tensor_tensor(
-                        page[n][:].indirect(entries(lst2, BANK * half, BANK)), h[:, cols], wgs_sb[:, cols], MULT
+                        page[n][:].indirect(entries(lst2, BANK * half, BANK)), larger, wgs_sb[:, cols], MULT
                     )
+            if n == 2:
+                turn(1, pick(1, 0, BANK, mid.tile([P, BANK], F32, name="picked1", offset=0, align_bytes=64))[:], 0, BANK)
+                turn(0, pick(0, 0, NP, mid.tile([P, NP], F32, name="picked0", offset=2048, align_bytes=64))[:], 0, NP)
+            if n == 3:
+                turn(2, pick(2, 0, NP, keep.tile([P, NP], F32, name="picked2", tag="flap_sb3", align_bytes=64))[:], 0, NP)
             if n > 0:
-                turn(n - 1, pick(n - 1, 0, NP, f"flap_sb{n}")[:], 0, NP)
                 nc.vector.tensor_tensor(page[n][:].indirect(lst2[:]), h[:], wgs_sb[:], MULT)
-                make_factor(n - 1, nc.gpsimd, keep.tile([P, NP], F32, name="factor", tag=f"h{n}", align_bytes=64))
+            for m, tag in {1: ((0, "h1"), (1, "h0")), 2: ((2, "h2"),), 3: ((3, "h3"),)}.get(n, ()):
+                make_factor(m, nc.gpsimd, keep.tile([P, NP], F32, name="factor", tag=tag, align_bytes=64))
 
         w2_woven = held([P, H, 4], BF16, "w2_woven")
         nc.scalar.copy(w2_woven[:], w2_raw[:].rearrange("p j c -> p c j"))
@@ -234,15 +240,15 @@ def tile_list_pitch_bearing_register_kernel(
                 x_woven[:].rearrange("p j t -> p (j t)"),
             )
 
-        picked = [pick(last, first, count, f"picked{first}") for first, count in ((0, QUARTER), (QUARTER, QUARTER), (BANK, BANK))]
+        picked = [pick(last, first, count, held([P, count], F32, f"picked3_{first}")) for first, count in ((0, QUARTER), (QUARTER, QUARTER), (BANK, BANK))]
         w2_q = keep.tile([P, H], U32, name="w2_q", tag="wgs_sb", align_bytes=64)
         w2_sc = held([P, H], U8, "w2_sc")
         nc.vector.quantize_mx(w2_q[:].bitcast(FP8X4), w2_sc[:], w2_woven[:].rearrange("p c j -> p (c j)"))
         turn(last, picked[0][:], 0, QUARTER)
         turn_back(0, late.tile([P, QUARTER, 4], BF16, name="x_woven0", offset=0, align_bytes=64))
+        picked_late = pick(1, BANK, BANK, late.tile([P, BANK], F32, name="picked_late", offset=1024, align_bytes=64))
         turn(last, picked[1][:], QUARTER, QUARTER)
-        turn_back(QUARTER, held([P, QUARTER, 4], BF16, "x_woven1"))
-        make_factor(last, nc.vector, late.tile([P, NP], F32, name="factor3", offset=1024, align_bytes=64))
+        turn_back(QUARTER, late.tile([P, QUARTER, 4], BF16, name="x_woven1", offset=4096, align_bytes=64))
 
         y_sb = [held([P, NP], F32, f"y{n}") for n in range(TILES)]
 
@@ -265,20 +271,25 @@ def tile_list_pitch_bearing_register_kernel(
         def store(n):
             nc.sync.dma_start(out=out[rows(n), :], in_=page[n][:])
 
-        for first in (0, QUARTER):
-            for n in (0, 1):
-                score(n, first, QUARTER, ("edge0", "flap0")[n] if first == 0 else ("edge1", "flap1")[n])
-                put(n, first, QUARTER)
-        turn(last, picked[2][:], BANK, BANK, late.tile([P, BANK], BF16, name="size_late", offset=0, align_bytes=64))
+        score(0, 0, QUARTER, "edge0")
+        put(0, 0, QUARTER)
+        score(1, 0, BANK, "flap0")
+        put(1, 0, BANK)
+        score(0, QUARTER, QUARTER, "edge1")
+        turn(last, picked[2][:], BANK, BANK, late.tile([P, BANK], BF16, name="size_late3", offset=0, align_bytes=64))
+        turn(1, picked_late[:], BANK, BANK, late.tile([P, BANK], BF16, name="size_late1", offset=4096, align_bytes=64))
         for first in (BANK, BANK + QUARTER):
             turn_back(first, held([P, QUARTER, 4], BF16, f"x_woven{first}"))
         score(2, 0, BANK, "back1")
         put(2, 0, BANK)
-        for n in range(3):
-            score(n, BANK, BANK, ("edge0", "flap0", "edge1")[n])
+        score(0, BANK, BANK, "flap1")
+        put(0, QUARTER, NP - QUARTER)
+        store(0)
+        for n in (1, 2):
+            score(n, BANK, BANK, ("edge0", "flap0")[n - 1])
             put(n, BANK, BANK)
             store(n)
-        score(3, 0, BANK, "flap1")
+        score(3, 0, BANK, "edge1")
         score(3, BANK, BANK, "back0")
         put(3, 0, NP)
         store(3)

@@ -34,6 +34,7 @@ def tile_list_pitch_bearing_register_kernel(
         keep = ctx.enter_context(tc.tile_pool(name="keep", bufs=1))
         late = ctx.enter_context(tc.tile_pool(name="late", bufs=1))
         mid = ctx.enter_context(tc.tile_pool(name="mid", bufs=1))
+        after = ctx.enter_context(tc.tile_pool(name="after", bufs=1))
         ring = ctx.enter_context(tc.tile_pool(name="ring", bufs=2))
         psum = ctx.enter_context(tc.psum_pool(name="psum", bufs=1))
 
@@ -69,7 +70,7 @@ def tile_list_pitch_bearing_register_kernel(
         w1_raw = [held([P, PASSES, 4, P * (hi - lo)], F32, f"w1_raw{lo}") for lo, hi in w1_groups]
         w4_w = held([P, PASSES, 2 * H], U8, "w4_w")
         page = [held([P, T2], F32, f"page{n}") for n in range(TILES)]
-        wgs_sb = keep.tile([P, S], F32, name="wgs_sb", tag="wgs_sb", align_bytes=64)
+        wgs_sb = after.tile([P, S], F32, name="wgs_sb", offset=0, align_bytes=64)
         wgo_sb = held([P, NP], F32, "wgo_sb")
         expo_sb = [held([P, NP], F32, f"expo{n}") for n in range(TILES)]
         w2_raw = held([P, 4, H], F32, "w2_raw")
@@ -212,7 +213,7 @@ def tile_list_pitch_bearing_register_kernel(
                 turn(1, pick(1, 0, BANK, mid.tile([P, BANK], F32, name="picked1", offset=0, align_bytes=64))[:], 0, BANK)
                 turn(0, pick(0, 0, NP, mid.tile([P, NP], F32, name="picked0", offset=2048, align_bytes=64))[:], 0, NP)
             if n == 3:
-                turn(2, pick(2, 0, NP, keep.tile([P, NP], F32, name="picked2", tag="flap_sb3", align_bytes=64))[:], 0, NP)
+                turn(2, pick(2, 0, BANK, keep.tile([P, BANK], F32, name="picked2", tag="flap_sb3", align_bytes=64))[:], 0, BANK)
             if n > 0:
                 nc.vector.tensor_tensor(page[n][:].indirect(lst2[:]), h[:], wgs_sb[:], MULT)
             for m, tag in {1: ((0, "h1"), (1, "h0")), 2: ((2, "h2"),), 3: ((3, "h3"),)}.get(n, ()):
@@ -231,24 +232,31 @@ def tile_list_pitch_bearing_register_kernel(
                 for u in range(2):
                     nc.tensor.transpose(back[:, b, u, :], x_t[:, first // P + b, u, :], ident_f32[:])
             nc.scalar.copy(
-                x_woven[:].bitcast(F32).rearrange("p (b j) u -> p b j u", j=P),
+                x_woven.bitcast(F32).rearrange("p (b j) u -> p b j u", j=P),
                 back[:].rearrange("p b u j -> p b j u"),
             )
+
+        def quantise_x(first, count, x_woven):
             nc.vector.quantize_mx(
-                x_q[:, first : first + QUARTER].bitcast(FP8X4),
-                x_sc[:, first : first + QUARTER],
+                x_q[:, first : first + count].bitcast(FP8X4),
+                x_sc[:, first : first + count],
                 x_woven[:].rearrange("p j t -> p (j t)"),
             )
 
         picked = [pick(last, first, count, held([P, count], F32, f"picked3_{first}")) for first, count in ((0, QUARTER), (QUARTER, QUARTER), (BANK, BANK))]
-        w2_q = keep.tile([P, H], U32, name="w2_q", tag="wgs_sb", align_bytes=64)
+        picked_late2 = pick(2, BANK, BANK, after.tile([P, BANK], F32, name="picked_late2", offset=2048, align_bytes=64))
+        w2_q = after.tile([P, H], U32, name="w2_q", offset=0, align_bytes=64)
         w2_sc = held([P, H], U8, "w2_sc")
         nc.vector.quantize_mx(w2_q[:].bitcast(FP8X4), w2_sc[:], w2_woven[:].rearrange("p c j -> p (c j)"))
         turn(last, picked[0][:], 0, QUARTER)
-        turn_back(0, late.tile([P, QUARTER, 4], BF16, name="x_woven0", offset=0, align_bytes=64))
+        x_woven0 = late.tile([P, QUARTER, 4], BF16, name="x_woven0", offset=0, align_bytes=64)
+        turn_back(0, x_woven0[:])
+        quantise_x(0, QUARTER, x_woven0)
         picked_late = pick(1, BANK, BANK, late.tile([P, BANK], F32, name="picked_late", offset=1024, align_bytes=64))
         turn(last, picked[1][:], QUARTER, QUARTER)
-        turn_back(QUARTER, late.tile([P, QUARTER, 4], BF16, name="x_woven1", offset=4096, align_bytes=64))
+        x_woven1 = late.tile([P, QUARTER, 4], BF16, name="x_woven1", offset=4096, align_bytes=64)
+        turn_back(QUARTER, x_woven1[:])
+        quantise_x(QUARTER, QUARTER, x_woven1)
 
         y_sb = [held([P, NP], F32, f"y{n}") for n in range(TILES)]
 
@@ -273,23 +281,23 @@ def tile_list_pitch_bearing_register_kernel(
 
         score(0, 0, QUARTER, "edge0")
         put(0, 0, QUARTER)
-        score(1, 0, BANK, "flap0")
-        put(1, 0, BANK)
+        for n in (1, 2):
+            score(n, 0, BANK, ("flap0", "flap1")[n - 1])
+            put(n, 0, BANK)
         score(0, QUARTER, QUARTER, "edge1")
         turn(last, picked[2][:], BANK, BANK, late.tile([P, BANK], BF16, name="size_late3", offset=0, align_bytes=64))
-        turn(1, picked_late[:], BANK, BANK, late.tile([P, BANK], BF16, name="size_late1", offset=4096, align_bytes=64))
+        turn(2, picked_late2[:], BANK, BANK, late.tile([P, BANK], BF16, name="size_late2", offset=4096, align_bytes=64))
+        turn(1, picked_late[:], BANK, BANK, late.tile([P, BANK], BF16, name="size_late1", offset=5120, align_bytes=64))
+        x_late = held([P, BANK, 4], BF16, "x_late")
         for first in (BANK, BANK + QUARTER):
-            turn_back(first, held([P, QUARTER, 4], BF16, f"x_woven{first}"))
-        score(2, 0, BANK, "back1")
-        put(2, 0, BANK)
-        score(0, BANK, BANK, "flap1")
+            turn_back(first, x_late[:, first - BANK : first - BANK + QUARTER, :])
+        quantise_x(BANK, BANK, x_late)
+        score(3, 0, BANK, "back1")
+        put(3, 0, BANK)
+        score(0, BANK, BANK, "edge0")
         put(0, QUARTER, NP - QUARTER)
         store(0)
-        for n in (1, 2):
-            score(n, BANK, BANK, ("edge0", "flap0")[n - 1])
+        for n in (1, 2, 3):
+            score(n, BANK, BANK, ("flap0", "flap1", "edge1")[n - 1])
             put(n, BANK, BANK)
             store(n)
-        score(3, 0, BANK, "edge1")
-        score(3, BANK, BANK, "back0")
-        put(3, 0, NP)
-        store(3)

@@ -33,7 +33,6 @@ def tile_list_pitch_bearing_register_kernel(
     with ExitStack() as ctx:
         keep = ctx.enter_context(tc.tile_pool(name="keep", bufs=1))
         late = ctx.enter_context(tc.tile_pool(name="late", bufs=1))
-        mid = ctx.enter_context(tc.tile_pool(name="mid", bufs=1))
         after = ctx.enter_context(tc.tile_pool(name="after", bufs=1))
         ring = ctx.enter_context(tc.tile_pool(name="ring", bufs=2))
         psum = ctx.enter_context(tc.psum_pool(name="psum", bufs=1))
@@ -172,10 +171,7 @@ def tile_list_pitch_bearing_register_kernel(
 
         for n in range(TILES):
             h = keep.tile([P, S], F32, name="h", tag=f"h{n}", align_bytes=64)
-            if n == 2:
-                flap_sb = mid.tile([P, S], F32, name="flap_sb2", offset=0, align_bytes=64)
-            else:
-                flap_sb = keep.tile([P, S], F32, name="flap_sb", tag=f"flap_sb{n}", align_bytes=64)
+            flap_sb = keep.tile([P, S], F32, name="flap_sb", tag=f"flap_sb{n}", align_bytes=64)
             for half in range(2):
                 cols = slice(BANK * half, BANK * (half + 1))
                 pair = 0 if n == 0 else 1 - half
@@ -209,15 +205,12 @@ def tile_list_pitch_bearing_register_kernel(
                     nc.vector.tensor_tensor(
                         page[n][:].indirect(entries(lst2, BANK * half, BANK)), larger, wgs_sb[:, cols], MULT
                     )
-            if n == 2:
-                turn(1, pick(1, 0, BANK, mid.tile([P, BANK], F32, name="picked1", offset=0, align_bytes=64))[:], 0, BANK)
-                turn(0, pick(0, 0, NP, mid.tile([P, NP], F32, name="picked0", offset=2048, align_bytes=64))[:], 0, NP)
-            if n == 3:
-                turn(2, pick(2, 0, BANK, keep.tile([P, BANK], F32, name="picked2", tag="flap_sb3", align_bytes=64))[:], 0, BANK)
             if n > 0:
+                count = BANK if n == 1 else NP
+                early = keep.tile([P, count], F32, name="early", tag=f"flap_sb{n}", align_bytes=64)
+                turn(n - 1, pick(n - 1, 0, count, early)[:], 0, count)
                 nc.vector.tensor_tensor(page[n][:].indirect(lst2[:]), h[:], wgs_sb[:], MULT)
-            for m, tag in {1: ((0, "h1"), (1, "h0")), 2: ((2, "h2"),), 3: ((3, "h3"),)}.get(n, ()):
-                make_factor(m, nc.gpsimd, keep.tile([P, NP], F32, name="factor", tag=tag, align_bytes=64))
+                make_factor(n - 1, nc.gpsimd, keep.tile([P, NP], F32, name="factor", tag=f"h{n}", align_bytes=64))
 
         w2_woven = held([P, H, 4], BF16, "w2_woven")
         nc.scalar.copy(w2_woven[:], w2_raw[:].rearrange("p j c -> p c j"))
@@ -244,7 +237,7 @@ def tile_list_pitch_bearing_register_kernel(
             )
 
         picked = [pick(last, first, count, held([P, count], F32, f"picked3_{first}")) for first, count in ((0, QUARTER), (QUARTER, QUARTER), (BANK, BANK))]
-        picked_late2 = pick(2, BANK, BANK, after.tile([P, BANK], F32, name="picked_late2", offset=2048, align_bytes=64))
+        picked_late = pick(0, BANK, BANK, after.tile([P, BANK], F32, name="picked_late", offset=2048, align_bytes=64))
         w2_q = after.tile([P, H], U32, name="w2_q", offset=0, align_bytes=64)
         w2_sc = held([P, H], U8, "w2_sc")
         nc.vector.quantize_mx(w2_q[:].bitcast(FP8X4), w2_sc[:], w2_woven[:].rearrange("p c j -> p (c j)"))
@@ -252,9 +245,9 @@ def tile_list_pitch_bearing_register_kernel(
         x_woven0 = late.tile([P, QUARTER, 4], BF16, name="x_woven0", offset=0, align_bytes=64)
         turn_back(0, x_woven0[:])
         quantise_x(0, QUARTER, x_woven0)
-        picked_late = pick(1, BANK, BANK, late.tile([P, BANK], F32, name="picked_late", offset=1024, align_bytes=64))
+        make_factor(last, nc.vector, late.tile([P, NP], F32, name="factor3", offset=1024, align_bytes=64))
         turn(last, picked[1][:], QUARTER, QUARTER)
-        x_woven1 = late.tile([P, QUARTER, 4], BF16, name="x_woven1", offset=4096, align_bytes=64)
+        x_woven1 = late.tile([P, QUARTER, 4], BF16, name="x_woven1", offset=5120, align_bytes=64)
         turn_back(QUARTER, x_woven1[:])
         quantise_x(QUARTER, QUARTER, x_woven1)
 
@@ -286,8 +279,7 @@ def tile_list_pitch_bearing_register_kernel(
             put(n, 0, BANK)
         score(0, QUARTER, QUARTER, "edge1")
         turn(last, picked[2][:], BANK, BANK, late.tile([P, BANK], BF16, name="size_late3", offset=0, align_bytes=64))
-        turn(2, picked_late2[:], BANK, BANK, late.tile([P, BANK], BF16, name="size_late2", offset=4096, align_bytes=64))
-        turn(1, picked_late[:], BANK, BANK, late.tile([P, BANK], BF16, name="size_late1", offset=5120, align_bytes=64))
+        turn(0, picked_late[:], BANK, BANK, late.tile([P, BANK], BF16, name="size_late0", offset=5120, align_bytes=64))
         x_late = held([P, BANK, 4], BF16, "x_late")
         for first in (BANK, BANK + QUARTER):
             turn_back(first, x_late[:, first - BANK : first - BANK + QUARTER, :])

from contextlib import ExitStack

import concourse.mybir as mybir
from concourse.masks import make_identity

K, T, S, H, T2, NP = 1024, 2048, 1024, 512, 2048, 1024
FLOPS = 2 * (2 * K * H * S + H * H * NP)

F32 = mybir.dt.float32
BF16 = mybir.dt.bfloat16
I32 = mybir.dt.int32
U32 = mybir.dt.uint32
U16 = mybir.dt.uint16
U8 = mybir.dt.uint8
FP8X4 = mybir.dt.float8_e4m3fn_x4
FP4X4 = mybir.dt.float4_e2m1fn_x4
MULT = mybir.AluOpType.mult
MAX = mybir.AluOpType.max
ABS = mybir.ActivationFunctionType.Abs

P = 128
PASSES = K // 512
TILES = H // P
BANK = 512
QUARTER = 256


def tile_list_pitch_bearing_register_kernel(
    tc, tab_words, tab_scales, offs, w1, w4_words, w4_scales, page0, wgs, offs2,
    shift, offs3, w2, expo, wgo, offs4, out,
):
    nc = tc.nc
    with ExitStack() as ctx:
        keep = ctx.enter_context(tc.tile_pool(name="keep", bufs=1))
        late = ctx.enter_context(tc.tile_pool(name="late", bufs=1))
        after = ctx.enter_context(tc.tile_pool(name="after", bufs=1))
        ring = ctx.enter_context(tc.tile_pool(name="ring", bufs=2))
        psum = ctx.enter_context(tc.psum_pool(name="psum", bufs=1))

        def held(shape, dtype, name):
            return keep.tile(shape, dtype, name=name, align_bytes=64)

        def bank(shape, dtype, tag):
            return psum.tile(shape, dtype, name=tag, tag=tag)

        def entries(lst, first, count):
            return lst[:, first // 16 : (first + count) // 16]

        lst1 = keep.tile([P, S // 16], U16, name="lst1")
        lst2 = keep.tile([P, S // 16], U16, name="lst2")
        lst3 = keep.tile([P, NP // 16], U16, name="lst3")
        lst4 = keep.tile([P, NP // 16], U16, name="lst4")

        tab_sc = held([P, T], U8, "tab_sc")
        w4_sc = held([P, PASSES, H], U8, "w4_sc")
        v_sc1 = held([P, S], U8, "v_sc1")
        nc.gpsimd.memset(tab_sc[:].bitcast(I32), 0)
        nc.vector.memset(w4_sc[:].rearrange("p a c -> p (a c)").bitcast(I32), 0)

        ident_bf = held([P, P], BF16, "ident_bf")
        ident_f32 = held([P, P], F32, "ident_f32")
        make_identity(nc, ident_f32[:])
        nc.scalar.activation(ident_bf[:], ident_f32[:], ABS)
        nc.gpsimd.memset(v_sc1[:].bitcast(I32), 0)

        tab = [held([P, T], U32, f"tab{a}") for a in range(PASSES)]
        w1_k = w1.rearrange("(a p j) c -> a p j c", p=P, j=4)
        w1_groups = ((0, 1), (1, 2), (2, 4))
        w1_raw = [held([P, PASSES, 4, P * (hi - lo)], F32, f"w1_raw{lo}") for lo, hi in w1_groups]
        w4_w = held([P, PASSES, 2 * H], U8, "w4_w")
        page = [held([P, T2], F32, f"page{n}") for n in range(TILES)]
        wgs_sb = after.tile([P, S], F32, name="wgs_sb", offset=0, align_bytes=64)
        wgo_sb = held([P, NP], F32, "wgo_sb")
        expo_sb = [held([P, NP], F32, f"expo{n}") for n in range(TILES)]
        w2_raw = held([P, 4, H], F32, "w2_raw")
        shift_sb = held([P, TILES], F32, "shift_sb")

        def load_w1(g):
            lo, hi = w1_groups[g]
            for a in range(PASSES):
                nc.sync.dma_start(out=w1_raw[g][:, a], in_=w1_k[a][:, :, P * lo : P * hi])

        def rows(n):
            return slice(P * n, P * (n + 1))

        nc.sync.dma_start(lst1[:], offs)
        nc.sync.dma_start(lst2[:], offs2)
        nc.sync.dma_start(lst3[:], offs3)

        def load_tab(a):
            nc.sync.dma_start(
                out=tab[a][:].bitcast(I32),
                in_=tab_words[a].rearrange("p t i -> p (t i)").bitcast(I32),
            )

        for q in range(4):
            nc.sync.dma_start(
                out=tab_sc[32 * q : 32 * q + 8, :].bitcast(I32),
                in_=tab_scales[:, 4 * q : 4 * q + 4, :].bitcast(I32),
            )
        v_sc = held([P, S], U8, "v_sc")
        nc.vector.tensor_copy(v_sc[:], tab_sc[:].indirect(lst1[:]))
        load_tab(0)
        load_w1(0)
        nc.sync.dma_start(out=w4_w[:].bitcast(I32), in_=w4_words.rearrange("a p c -> p a c").bitcast(I32))
        for q in range(4):
            nc.sync.dma_start(
                out=w4_sc[32 * q : 32 * q + 4, :, :].bitcast(I32),
                in_=w4_scales[:, 4 * q : 4 * q + 4, :].rearrange("a r c -> r a c").bitcast(I32),
            )
        load_tab(1)
        nc.sync.dma_start(out=v_sc1[0:100, :].bitcast(I32), in_=v_sc[4:104, :].bitcast(I32))
        nc.sync.dma_start(out=page[0][:], in_=page0[rows(0), :])
        nc.sync.dma_start(out=wgs_sb[:, :BANK], in_=wgs[:, :BANK])
        load_w1(1)
        load_w1(2)
        nc.sync.dma_start(out=wgs_sb[:, BANK:], in_=wgs[:, BANK:])
        nc.sync.dma_start(out=page[1][:], in_=page0[rows(1), :])
        nc.sync.dma_start(out=page[2][:], in_=page0[rows(2), :])
        with nc.allow_non_contiguous_dma(reason="one shift value to a partition"):
            nc.sync.dma_start(out=shift_sb[:], in_=shift.rearrange("(n p) -> p n", p=P))
        nc.sync.dma_start(out=w2_raw[:], in_=w2.rearrange("(p j) c -> p j c", j=4))
        nc.sync.dma_start(out=wgo_sb[:], in_=wgo)
        for n in range(TILES):
            nc.sync.dma_start(out=expo_sb[n][:], in_=expo[rows(n), :])
        nc.sync.dma_start(lst4[:], offs4)
        nc.sync.dma_start(out=page[3][:], in_=page0[rows(3), :])

        v_w = [held([P, S], U32, f"v_w{a}") for a in range(PASSES)]
        nc.vector.tensor_copy(v_w[0][:], tab[0][:].indirect(lst1[:]))

        w1_q, w1_sc = [], []
        for n in range(TILES):
            g = min(n, 2)
            first = P * (n - w1_groups[g][0])
            woven = keep.tile([P, PASSES, P, 4], BF16, name="woven", tag=f"w1_woven{n}", align_bytes=64)
            nc.scalar.copy(woven[:], w1_raw[g][:, :, :, first : first + P].rearrange("p a j c -> p a c j"))
            codes = held([P, PASSES * P], U32, f"w1_q{n}")
            scales = held([P, PASSES * P], U8, f"w1_sc{n}")
            nc.vector.quantize_mx(codes[:].bitcast(FP8X4), scales[:], woven[:].rearrange("p a c j -> p (a c j)"))
            w1_q.append([codes[:, rows(a)] for a in range(PASSES)])
            w1_sc.append([scales[:, rows(a)] for a in range(PASSES)])
            if n == 0:
                for first in (0, BANK):
                    nc.vector.tensor_copy(v_w[1][:, first : first + BANK], tab[1][:].indirect(entries(lst1, first, BANK)))

        x_t = held([P, NP // P, 2, P], F32, "x_t")
        weight_y = {}

        def turn(n, picked, first, count, size=None):
            blocks = count // P
            if size is None:
                size = ring.tile([P, count], BF16, name="size", tag=f"size{count}", align_bytes=64)
            nc.scalar.activation(size[:], picked, ABS, bias=shift_sb[:, n : n + 1])
            turned = psum.tile([P, blocks, P], BF16, name="turned", tag="turned", bufs=2)
            for b in range(blocks):
                nc.tensor.transpose(turned[:, b, :], size[:, P * b : P * (b + 1)], ident_bf[:])
            nc.scalar.copy(
                x_t[:, first // P : first // P + blocks, :, 32 * n : 32 * (n + 1)],
                turned[:].bitcast(F32).rearrange("j b (m u) -> j b u m", u=2),
            )

        def pick(n, first, count, picked):
            lst = lst3[:] if count == NP else entries(lst3, first, count)
            nc.vector.tensor_copy(picked[:], page[n][:].indirect(lst))
            return picked

        def make_factor(n, engine, factor):
            engine.tensor_tensor(factor[:], expo_sb[n][:], wgo_sb[:], MULT)
            weight_y[n] = factor

        for n in range(TILES):
            h = keep.tile([P, S], F32, name="h", tag=f"h{n}", align_bytes=64)
            flap_sb = keep.tile([P, S], F32, name="flap_sb", tag=f"flap_sb{n}", align_bytes=64)
            for half in range(2):
                cols = slice(BANK * half, BANK * (half + 1))
                pair = 0 if n == 0 else 1 - half
                edge = bank([P, BANK], F32, f"edge{pair}")
                flap = bank([P, BANK], F32, f"flap{pair}")
                for a in range(PASSES):
                    nc.tensor.matmul_mx(
                        out=flap[:],
                        lhsT=w1_q[n][a].bitcast(FP8X4),
                        lhsT_scale=w1_sc[n][a],
                        rhs=v_w[a][:, cols].bitcast(FP8X4),
                        rhs_scale=v_sc[4 * a :, cols],
                        start=(a == 0), stop=(a == PASSES - 1),
                    )
                for a in range(PASSES):
                    nc.tensor.matmul_mx(
                        out=edge[:],
                        lhsT=w4_w[:, a, 2 * P * n : 2 * P * (n + 1)].bitcast(FP4X4),
                        lhsT_scale=w4_sc[:, a, rows(n)],
                        rhs=v_w[a][:, cols].bitcast(FP8X4),
                        rhs_scale=(v_sc, v_sc1)[a][:, cols],
                        start=(a == 0), stop=(a == PASSES - 1),
                    )
                nc.scalar.copy(flap_sb[:, cols], flap[:])
                larger = h[:, cols]
                if (n, half) == (0, 1):
                    h_late = keep.tile([P, BANK], F32, name="h_late", tag="w1_woven1", align_bytes=64)
                    larger = h_late[:]
                nc.vector.tensor_tensor(larger, edge[:], flap_sb[:, cols], MAX)
                if n == 0:
                    nc.vector.tensor_tensor(
                        page[n][:].indirect(entries(lst2, BANK * half, BANK)), larger, wgs_sb[:, cols], MULT
                    )
            if n > 0:
                count = BANK if n == 1 else NP
                early = keep.tile([P, count], F32, name="early", tag=f"flap_sb{n}", align_bytes=64)
                turn(n - 1, pick(n - 1, 0, count, early)[:], 0, count)
                nc.vector.tensor_tensor(page[n][:].indirect(lst2[:]), h[:], wgs_sb[:], MULT)
                make_factor(n - 1, nc.gpsimd, keep.tile([P, NP], F32, name="factor", tag=f"h{n}", align_bytes=64))

        w2_woven = held([P, H, 4], BF16, "w2_woven")
        nc.scalar.copy(w2_woven[:], w2_raw[:].rearrange("p j c -> p c j"))

        last = TILES - 1
        x_q = held([P, NP], U32, "x_q")
        x_sc = held([P, NP], U8, "x_sc")

        def turn_back(first, x_woven):
            back = bank([P, QUARTER // P, 2, P], F32, f"back{first // QUARTER % 2}")
            for b in range(QUARTER // P):
                for u in range(2):
                    nc.tensor.transpose(back[:, b, u, :], x_t[:, first // P + b, u, :], ident_f32[:])
            nc.scalar.copy(
                x_woven.bitcast(F32).rearrange("p (b j) u -> p b j u", j=P),
                back[:].rearrange("p b u j -> p b j u"),
            )

        def quantise_x(first, count, x_woven):
            nc.vector.quantize_mx(
                x_q[:, first : first + count].bitcast(FP8X4),
                x_sc[:, first : first + count],
                x_woven[:].rearrange("p j t -> p (j t)"),
            )

        picked = [pick(last, first, count, held([P, count], F32, f"picked3_{first}")) for first, count in ((0, QUARTER), (QUARTER, QUARTER), (BANK, BANK))]
        picked_late = pick(0, BANK, BANK, after.tile([P, BANK], F32, name="picked_late", offset=2048, align_bytes=64))
        w2_q = after.tile([P, H], U32, name="w2_q", offset=0, align_bytes=64)
        w2_sc = held([P, H], U8, "w2_sc")
        nc.vector.quantize_mx(w2_q[:].bitcast(FP8X4), w2_sc[:], w2_woven[:].rearrange("p c j -> p (c j)"))
        turn(last, picked[0][:], 0, QUARTER)
        x_woven0 = late.tile([P, QUARTER, 4], BF16, name="x_woven0", offset=0, align_bytes=64)
        turn_back(0, x_woven0[:])
        quantise_x(0, QUARTER, x_woven0)
        make_factor(last, nc.vector, late.tile([P, NP], F32, name="factor3", offset=1024, align_bytes=64))
        turn(last, picked[1][:], QUARTER, QUARTER)
        x_woven1 = late.tile([P, QUARTER, 4], BF16, name="x_woven1", offset=5120, align_bytes=64)
        turn_back(QUARTER, x_woven1[:])
        quantise_x(QUARTER, QUARTER, x_woven1)

        y_sb = [held([P, NP], F32, f"y{n}") for n in range(TILES)]

        def score(n, first, count, tag):
            cols = slice(first, first + count)
            acc = bank([P, count], F32, tag)
            nc.tensor.matmul_mx(
                out=acc[:],
                lhsT=w2_q[:, rows(n)].bitcast(FP8X4), lhsT_scale=w2_sc[:, rows(n)],
                rhs=x_q[:, cols].bitcast(FP8X4), rhs_scale=x_sc[:, cols],
                start=True, stop=True,
            )
            nc.scalar.copy(y_sb[n][:, cols], acc[:])

        def put(n, first, count):
            cols = slice(first, first + count)
            lst = lst4[:] if count == NP else entries(lst4, first, count)
            nc.vector.tensor_tensor(page[n][:].indirect(lst), y_sb[n][:, cols], weight_y[n][:, cols], MULT)

        def store(n):
            nc.sync.dma_start(out=out[rows(n), :], in_=page[n][:])

        score(0, 0, QUARTER, "edge0")
        put(0, 0, QUARTER)
        for n in (1, 2):
            score(n, 0, BANK, ("flap0", "flap1")[n - 1])
            put(n, 0, BANK)
        score(0, QUARTER, QUARTER, "edge1")
        turn(last, picked[2][:], BANK, BANK, late.tile([P, BANK], BF16, name="size_late3", offset=0, align_bytes=64))
        turn(0, picked_late[:], BANK, BANK, late.tile([P, BANK], BF16, name="size_late0", offset=5120, align_bytes=64))
        x_late = held([P, BANK, 4], BF16, "x_late")
        for first in (BANK, BANK + QUARTER):
            turn_back(first, x_late[:, first - BANK : first - BANK + QUARTER, :])
        quantise_x(BANK, BANK, x_late)
        score(3, 0, BANK, "back1")
        put(3, 0, BANK)
        score(0, BANK, BANK, "edge0")
        put(0, QUARTER, NP - QUARTER)
        store(0)
        for n in (1, 2, 3):
            score(n, BANK, BANK, ("flap0", "flap1", "edge1")[n - 1])
            put(n, BANK, BANK)
            store(n)
